import numpy as np
import ml_dtypes


def mxq(x, axis, fmt="e4m3"):
    dtype, down = {"e4m3": (ml_dtypes.float8_e4m3fn, 7), "e5m2": (ml_dtypes.float8_e5m2, 14)}[fmt]
    v = np.moveaxis(np.asarray(x, np.float32).astype(ml_dtypes.bfloat16).astype(np.float64), axis, -1)
    blocks = v.reshape(v.shape[:-1] + (-1, 32))
    amax = np.abs(blocks).max(-1, keepdims=True)
    byte = np.maximum(np.where(amax > 0, np.frexp(amax)[1] - 1 + 127, 0) - down, 1)
    scale = np.exp2(byte - 127.0)
    codes = (blocks / scale).astype(np.float32).astype(dtype).astype(np.float64)
    return np.moveaxis((codes * scale).reshape(v.shape), -1, axis)


WIDE = False


def mx_kscale(k):
    if not WIDE:
        return np.ones(k)
    levels = np.array([10, -10, 5, -5, 0])
    if k % 512:
        return np.exp2(np.random.permutation(np.resize(levels, k // 32))).repeat(32)
    a = np.empty((k // 512, 16))
    for p in range(k // 512):
        a[p, :8] = np.random.permutation(np.resize(levels, 8))
        for g in range(8):
            far = levels[np.abs(levels - a[p, g]) >= 10]
            a[p, g + 8] = far[np.random.randint(len(far))]
    return np.exp2(a.ravel()).repeat(32)


def f64(x):
    return np.asarray(x).astype(np.float64)


def striped(idx):
    return np.tile(np.asarray(idx).reshape(-1, 16).T, (8, 1)).astype(np.uint16)


def unstriped(offs):
    return offs[:16].T.reshape(-1).astype(np.int64)


def striped8(idx):
    return np.asarray(idx).reshape(8, -1, 16).transpose(0, 2, 1).reshape(128, -1).astype(np.uint16)


def unstriped8(offs):
    return offs.reshape(8, 16, -1).transpose(0, 2, 1).reshape(8, -1).astype(np.int64)


def pick8(x, idx, run):
    r = np.arange(len(x))
    return x[r[:, None], idx[r % (8 * run) // run]]


E2M1 = np.array([0.0, 0.5, 1.0, 1.5, 2.0, 3.0, 4.0, 6.0, -0.0, -0.5, -1.0, -1.5, -2.0, -3.0, -4.0, -6.0])


def pack_weight(w, fmt):
    k, n = w.shape
    w = f64(np.asarray(w, np.float32).astype(ml_dtypes.bfloat16)).reshape(k // 32, 32, n)
    amax = np.abs(w).max(1)
    if fmt == "e4m3":
        byte = np.frexp(amax)[1] - 1 + 127 - 7
    else:
        mant, ex = np.frexp(amax / 6.0)
        byte = np.where(mant > 0.5, ex, ex - 1) + 127
    byte = np.clip(np.where(amax > 0, byte, 1), 1, 254)
    scaled = (w * np.exp2(127.0 - byte)[:, None, :]).reshape(k, n).astype(np.float32)
    by_word = np.ascontiguousarray(scaled.reshape(k // 512, 128, 4, n).transpose(0, 1, 3, 2))
    if fmt == "e4m3":
        words = by_word.astype(ml_dtypes.float8_e4m3fn).view(np.uint8)
    else:
        c = by_word.astype(ml_dtypes.float4_e2m1fn).view(np.uint8) & 0xF
        words = (c[..., 0::2] | (c[..., 1::2] << 4)).reshape(k // 512, 128, 2 * n)
    return np.ascontiguousarray(words), np.ascontiguousarray(byte.astype(np.uint8).reshape(k // 512, 16, n))


def unpack_weight(words, scales, fmt):
    g, _, n = scales.shape
    words = np.ascontiguousarray(words).reshape(g, 128, n, -1)
    if fmt == "e4m3":
        vals = words.view(ml_dtypes.float8_e4m3fn).astype(np.float64)
    else:
        nib = np.empty((g, 128, n, 4), np.uint8)
        nib[..., 0::2] = words & 0xF
        nib[..., 1::2] = words >> 4
        vals = E2M1[nib]
    vals = vals * np.repeat(np.exp2(scales.astype(np.float64) - 127.0), 8, axis=1)[..., None]
    return vals.transpose(0, 1, 3, 2).reshape(g * 512, n)


def sigmoid(v):
    return 1.0 / (1.0 + np.exp(-v))


K, R, F, T, J, M, G = 512, 128, 512, 2048, 512, 256, 32


def setup_inputs():
    n = np.random.standard_normal
    idx = np.random.permutation(T)[:J]
    idx2 = np.stack([np.random.permutation(J)[:M] for _ in range(8)])
    fk = mx_kscale(K)
    dtabp = pack_weight(n((K, T)) / fk[:, None], "e4m3")
    tabp = pack_weight(n((K, T)) / fk[:, None], "e4m3")
    return {
        "dtab_words": dtabp[0],
        "dtab_scales": dtabp[1],
        "tab_words": tabp[0],
        "tab_scales": tabp[1],
        "w1": (n((K, R)) * 1 / np.sqrt(K) * fk[:, None]).astype(np.float32),
        "gain": (np.random.uniform(0.5, 1.5, (R, 1))).astype(np.float32),
        "share": (np.random.uniform(0.4, 1.0, (R, 1))).astype(np.float32),
        "pb": (np.random.uniform(-0.5, 0.5, (1, M))).astype(np.float32),
        "og": (np.random.uniform(0.5, 2.0, (R, 1))).astype(np.float32),
        "base": (0.3 * n((R, M))).astype(np.float32),
        "offs": striped(idx),
        "offs2": striped8(idx2),
    }


def reference(dtab_words, dtab_scales, tab_words, tab_scales, w1, gain, share, pb, og, base, offs, offs2):
    idx = unstriped(offs)
    idx2 = unstriped8(offs2)
    dtabu = unpack_weight(dtab_words, dtab_scales, "e4m3")
    tabu = unpack_weight(tab_words, tab_scales, "e4m3")
    w1q = mxq(f64(w1), 0, "e4m3")
    tabidxg = tabu[:, idx]
    a = w1q.T @ tabidxg
    dtabidxg = dtabu[:, idx]
    ta = w1q.T @ dtabidxg
    h0 = np.tanh(a)
    h1 = h0 * f64(gain)
    s = pick8(h1, idx2, 16) + f64(pb)
    m1 = s.reshape(R, G, M // G).mean(axis=2)
    mr = np.repeat(m1, M // G, axis=1)
    xh0 = ta * (1.0 - np.square(h0))
    xh1 = xh0 * f64(gain)
    xs = pick8(xh1, idx2, 16)
    xm1 = xs.reshape(R, G, M // G).mean(axis=2)
    xmr = np.repeat(xm1, M // G, axis=1)
    xu1 = (xs - xmr * f64(share)) * sigmoid(s - mr * f64(share))
    y = xu1 * f64(og) + f64(base)
    return y

@@ -1,0 +1,198 @@
+from contextlib import ExitStack
+
+import concourse.mybir as mybir
+
+K, R, T, J, M, G = 512, 128, 2048, 512, 256, 32
+FLOPS = 2 * 2 * K * R * J
+
+F32 = mybir.dt.float32
+BF16 = mybir.dt.bfloat16
+I32 = mybir.dt.int32
+U32 = mybir.dt.uint32
+U16 = mybir.dt.uint16
+U8 = mybir.dt.uint8
+FP8X4 = mybir.dt.float8_e4m3fn_x4
+ALU = mybir.AluOpType
+ACT = mybir.ActivationFunctionType
+AXIS = mybir.AxisListType
+
+P = 128
+PACK = 4
+GROUP = M // G
+LIST_ROWS = 16
+TAB_PLANE = 0
+DTAB_PLANE = 4
+HALVES = 2
+
+
+def load_words(nc, tile, words):
+    nc.sync.dma_start(tile[:].bitcast(I32), words[0].rearrange("p n t -> p (n t)").bitcast(I32))
+
+
+def load_scales(nc, tile, scales, plane):
+    for q in range(4):
+        first = 32 * q + plane
+        nc.sync.dma_start(tile[first : first + 4, :].bitcast(I32), scales[0, 4 * q : 4 * q + 4, :].bitcast(I32))
+
+
+def tile_attend_tcpickcentred_kernel(
+    tc, dtab_words, dtab_scales, tab_words, tab_scales, w1, gain, share, pb, og, base, offs, offs2, out
+):
+    nc = tc.nc
+    with ExitStack() as ctx:
+        sb = ctx.enter_context(tc.tile_pool(name="sb", bufs=1))
+        ps = ctx.enter_context(tc.psum_pool(name="ps", bufs=1))
+
+        slots = sb.tile([P, J // LIST_ROWS], U16, name="slots")
+        picks = sb.tile([P, M // LIST_ROWS], U16, name="picks")
+        tab_w = sb.tile([P, T], U32, name="tab_w")
+        tab_s = sb.tile([P, T], U8, name="tab_s")
+        dtab_w = sb.tile([P, T], U32, name="dtab_w", tag="dtab_w")
+        dtab_s = sb.tile([P, T], U8, name="dtab_s", tag="dtab_s", align_bytes=64)
+        w_raw = sb.tile([P, PACK, R], F32, name="w_raw")
+        gain_c = sb.tile([P, 1], F32, name="gain_c")
+        share_c = sb.tile([P, 1], F32, name="share_c")
+        og_c = sb.tile([P, 1], F32, name="og_c")
+        pb_c = sb.tile([P, 2], F32, name="pb_c")
+        base_t = sb.tile([P, M], F32, name="base_t")
+        ident = sb.tile([P, P], F32, name="ident")
+
+        nc.gpsimd.memset(tab_s[:].bitcast(I32), 0)
+        nc.vector.memset(dtab_s[:].bitcast(I32), 0)
+
+        col_less_row = sb.tile([P, P], I32, name="col_less_row")
+        nc.gpsimd.iota(col_less_row[:], pattern=[[1, P]], base=0, channel_multiplier=-1)
+        nc.vector.tensor_scalar(ident[:], col_less_row[:], 0.0, None, ALU.is_equal)
+        nc.sync.dma_start(slots[:], offs)
+        nc.sync.dma_start(w_raw[:], w1.rearrange("(p j) r -> p j r", j=PACK))
+        nc.sync.dma_start(picks[:], offs2)
+        load_scales(nc, tab_s, tab_scales, TAB_PLANE)
+        load_words(nc, tab_w, tab_words)
+        load_scales(nc, dtab_s, dtab_scales, DTAB_PLANE)
+        load_words(nc, dtab_w, dtab_words)
+        nc.sync.dma_start(share_c[:], share)
+        nc.sync.dma_start(og_c[:], og)
+        nc.sync.dma_start(base_t[:], base)
+        nc.gpsimd.dma_start(pb_c[:], pb.rearrange("o (p c) -> p (o c)", c=2))
+        nc.gpsimd.dma_start(gain_c[:], gain)
+
+        w_bf = sb.tile([P, R, PACK], BF16, name="w_bf", align_bytes=64)
+        nc.vector.tensor_copy(w_bf[:], w_raw[:].rearrange("p j r -> p r j"))
+
+        pb_ps = ps.tile([P, 2, P], F32, name="pb_ps")
+        for c in range(2):
+            nc.tensor.transpose(pb_ps[:, c, :], pb_c[:, c : c + 1].to_broadcast([P, P]), ident[:])
+        pb_t = sb.tile([P, M], F32, name="pb_t")
+        nc.scalar.copy(pb_t[:].rearrange("p (n c) -> p n c", c=2), pb_ps[:].rearrange("p c n -> p n c"))
+
+        neg_gain = sb.tile([P, 1], F32, name="neg_gain")
+        nc.scalar.mul(neg_gain[:], gain_c[:], -1.0)
+
+        w_codes = sb.tile([P, R], U32, name="w_codes", align_bytes=64)
+        w_scales = sb.tile([P, R], U8, name="w_scales", align_bytes=64)
+
+        tab_gw = sb.tile([P, J], U32, name="tab_gw", align_bytes=64)
+        tab_gs = sb.tile([P, J], U8, name="tab_gs", align_bytes=64)
+        dtab_gw = sb.tile([P, J], U32, name="dtab_gw", align_bytes=64)
+        dtab_gs = sb.tile([P, J], U8, name="dtab_gs", align_bytes=64)
+
+        jh = J // HALVES
+        jc = jh // LIST_ROWS
+        nc.vector.quantize_mx(
+            out=w_codes[:].bitcast(FP8X4), scales=w_scales[:], in_=w_bf[:].rearrange("p r j -> p (r j)")
+        )
+        nc.vector.tensor_copy(tab_gs[:], tab_s[:].indirect(slots[:]))
+        h0 = sb.tile([P, J], F32, name="h0")
+        h1 = sb.tile([P, J], F32, name="h1")
+        for h in range(HALVES):
+            cols = slice(h * jh, (h + 1) * jh)
+            nc.vector.tensor_copy(tab_gw[:, cols], tab_w[:].indirect(slots[:, h * jc : (h + 1) * jc]))
+            a_ps = ps.tile([P, jh], F32, name="a_ps%d" % h)
+            nc.tensor.matmul_mx(
+                a_ps[:],
+                lhsT=w_codes[:].bitcast(FP8X4),
+                lhsT_scale=w_scales[:],
+                rhs=tab_gw[:, cols].bitcast(FP8X4),
+                rhs_scale=tab_gs[TAB_PLANE:P, cols],
+                start=True,
+                stop=True,
+            )
+            nc.scalar.activation(h0[:, cols], a_ps[:], ACT.Tanh)
+            nc.scalar.mul(h1[:, cols], h0[:, cols], gain_c[:])
+
+        h0_sq = sb.tile([P, J], F32, name="h0_sq")
+        slope = sb.tile([P, J], F32, name="slope")
+        nc.scalar.activation(h0_sq[:], h0[:], ACT.Square)
+        nc.scalar.activation(slope[:], h0_sq[:], ACT.Identity, bias=gain_c[:], scale=neg_gain[:])
+        centre = sb.tile([P, 1], F32, name="centre")
+        nc.scalar.mul(centre[:], share_c[:], -1.0 / GROUP)
+        half_og = sb.tile([P, 1], F32, name="half_og")
+        nc.scalar.mul(half_og[:], og_c[:], 0.5)
+
+        def grouped(t):
+            return t.rearrange("p (g e) -> p g e", e=GROUP)
+
+        nc.vector.tensor_copy(dtab_gs[:], dtab_s[:].indirect(slots[:]))
+        s = sb.tile([P, M], F32, name="s", tag="dtab_s", align_bytes=64)
+        nc.vector.tensor_tensor(s[:], h1[:].indirect(picks[:]), pb_t[:], ALU.add)
+        s_sum = sb.tile([P, G], F32, name="s_sum")
+        ta_ps = []
+        for h in range(HALVES):
+            slot_cols = slice(h * jh, (h + 1) * jh)
+            nc.vector.tensor_copy(dtab_gw[:, slot_cols], dtab_w[:].indirect(slots[:, h * jc : (h + 1) * jc]))
+            ta_ps.append(ps.tile([P, jh], F32, name="ta_ps%d" % h))
+            nc.tensor.matmul_mx(
+                ta_ps[h][:],
+                lhsT=w_codes[:].bitcast(FP8X4),
+                lhsT_scale=w_scales[:],
+                rhs=dtab_gw[:, slot_cols].bitcast(FP8X4),
+                rhs_scale=dtab_gs[DTAB_PLANE:P, slot_cols],
+                start=True,
+                stop=True,
+            )
+            if h == 0:
+                nc.vector.tensor_reduce(s_sum[:], grouped(s[:]), AXIS.X, ALU.add)
+
+        z = sb.tile([P, M], F32, name="z", tag="dtab_w")
+        nc.vector.scalar_tensor_tensor(
+            grouped(z[:]), s_sum[:].unsqueeze(2).to_broadcast([P, G, GROUP]), centre[:], grouped(s[:]), ALU.mult, ALU.add
+        )
+        th = sb.tile([P, M], F32, name="th")
+        nc.scalar.activation(th[:], z[:], ACT.Tanh, scale=0.5)
+
+        xh1 = sb.tile([P, J], F32, name="xh1")
+        for h in range(HALVES):
+            slot_cols = slice(h * jh, (h + 1) * jh)
+            nc.vector.tensor_tensor(xh1[:, slot_cols], ta_ps[h][:], slope[:, slot_cols], ALU.mult)
+
+        mh = M // HALVES
+        mc = mh // LIST_ROWS
+        gh = G // HALVES
+        cols = [slice(h * mh, (h + 1) * mh) for h in range(HALVES)]
+        grps = [slice(h * gh, (h + 1) * gh) for h in range(HALVES)]
+        xs = sb.tile([P, M], F32, name="xs")
+        xs_sum = sb.tile([P, G], F32, name="xs_sum")
+        xc = sb.tile([P, M], F32, name="xc")
+        xg = sb.tile([P, M], F32, name="xg")
+        res = sb.tile([P, M], F32, name="res")
+        for h in range(HALVES):
+            nc.vector.tensor_copy(xs[:, cols[h]], xh1[:].indirect(picks[:, h * mc : (h + 1) * mc]))
+        for h in range(HALVES):
+            nc.vector.tensor_reduce(xs_sum[:, grps[h]], grouped(xs[:, cols[h]]), AXIS.X, ALU.add)
+        for h in range(HALVES):
+            nc.vector.scalar_tensor_tensor(
+                grouped(xc[:, cols[h]]),
+                xs_sum[:, grps[h]].unsqueeze(2).to_broadcast([P, gh, GROUP]),
+                centre[:],
+                grouped(xs[:, cols[h]]),
+                ALU.mult,
+                ALU.add,
+            )
+        for h in range(HALVES):
+            nc.vector.scalar_tensor_tensor(xg[:, cols[h]], th[:, cols[h]], 1.0, xc[:, cols[h]], ALU.add, ALU.mult)
+        for h in range(HALVES):
+            nc.vector.scalar_tensor_tensor(
+                res[:, cols[h]], xg[:, cols[h]], half_og[:], base_t[:, cols[h]], ALU.mult, ALU.add
+            )
+            queue = nc.sync if h == 0 else nc.scalar
+            queue.dma_start(out[:, cols[h]], res[:, cols[h]])

@@ -1,6 +1,7 @@
 from contextlib import ExitStack
 
 import concourse.mybir as mybir
+from concourse.masks import make_identity
 
 K, R, T, J, M, G = 512, 128, 2048, 512, 256, 32
 FLOPS = 2 * 2 * K * R * J
@@ -29,10 +30,10 @@ def load_words(nc, tile, words):
     nc.sync.dma_start(tile[:].bitcast(I32), words[0].rearrange("p n t -> p (n t)").bitcast(I32))
 
 
-def load_scales(nc, tile, scales, plane):
-    for q in range(4):
+def load_scales(queues, tile, scales, plane):
+    for q, queue in enumerate(queues):
         first = 32 * q + plane
-        nc.sync.dma_start(tile[first : first + 4, :].bitcast(I32), scales[0, 4 * q : 4 * q + 4, :].bitcast(I32))
+        queue.dma_start(tile[first : first + 4, :].bitcast(I32), scales[0, 4 * q : 4 * q + 4, :].bitcast(I32))
 
 
 def tile_attend_tcpickcentred_kernel(
@@ -60,26 +61,24 @@ def tile_attend_tcpickcentred_kernel(
         nc.gpsimd.memset(tab_s[:].bitcast(I32), 0)
         nc.vector.memset(dtab_s[:].bitcast(I32), 0)
 
-        col_less_row = sb.tile([P, P], I32, name="col_less_row")
-        nc.gpsimd.iota(col_less_row[:], pattern=[[1, P]], base=0, channel_multiplier=-1)
-        nc.vector.tensor_scalar(ident[:], col_less_row[:], 0.0, None, ALU.is_equal)
+        make_identity(nc, ident[:])
         nc.sync.dma_start(slots[:], offs)
         nc.sync.dma_start(w_raw[:], w1.rearrange("(p j) r -> p j r", j=PACK))
-        nc.sync.dma_start(picks[:], offs2)
-        load_scales(nc, tab_s, tab_scales, TAB_PLANE)
+        nc.scalar.dma_start(pb_c[:], pb.rearrange("o (p c) -> p (o c)", c=2))
+        load_scales([nc.sync, nc.sync, nc.scalar, nc.scalar], tab_s, tab_scales, TAB_PLANE)
         load_words(nc, tab_w, tab_words)
-        load_scales(nc, dtab_s, dtab_scales, DTAB_PLANE)
+        nc.sync.dma_start(gain_c[:], gain)
+        load_scales([nc.sync] * 4, dtab_s, dtab_scales, DTAB_PLANE)
         load_words(nc, dtab_w, dtab_words)
+        nc.sync.dma_start(picks[:], offs2)
         nc.sync.dma_start(share_c[:], share)
         nc.sync.dma_start(og_c[:], og)
         nc.sync.dma_start(base_t[:], base)
-        nc.gpsimd.dma_start(pb_c[:], pb.rearrange("o (p c) -> p (o c)", c=2))
-        nc.gpsimd.dma_start(gain_c[:], gain)
 
         w_bf = sb.tile([P, R, PACK], BF16, name="w_bf", align_bytes=64)
         nc.vector.tensor_copy(w_bf[:], w_raw[:].rearrange("p j r -> p r j"))
 
-        pb_ps = ps.tile([P, 2, P], F32, name="pb_ps")
+        pb_ps = ps.tile([P, 2, P], F32, name="pb_ps", tag="bank0")
         for c in range(2):
             nc.tensor.transpose(pb_ps[:, c, :], pb_c[:, c : c + 1].to_broadcast([P, P]), ident[:])
         pb_t = sb.tile([P, M], F32, name="pb_t")
@@ -93,7 +92,6 @@ def tile_attend_tcpickcentred_kernel(
 
         tab_gw = sb.tile([P, J], U32, name="tab_gw", align_bytes=64)
         tab_gs = sb.tile([P, J], U8, name="tab_gs", align_bytes=64)
-        dtab_gw = sb.tile([P, J], U32, name="dtab_gw", align_bytes=64)
         dtab_gs = sb.tile([P, J], U8, name="dtab_gs", align_bytes=64)
 
         jh = J // HALVES
@@ -102,14 +100,14 @@ def tile_attend_tcpickcentred_kernel(
             out=w_codes[:].bitcast(FP8X4), scales=w_scales[:], in_=w_bf[:].rearrange("p r j -> p (r j)")
         )
         nc.vector.tensor_copy(tab_gs[:], tab_s[:].indirect(slots[:]))
+        a_ps = ps.tile([P, J], F32, name="a_ps", tag="bank0")
         h0 = sb.tile([P, J], F32, name="h0")
         h1 = sb.tile([P, J], F32, name="h1")
         for h in range(HALVES):
             cols = slice(h * jh, (h + 1) * jh)
             nc.vector.tensor_copy(tab_gw[:, cols], tab_w[:].indirect(slots[:, h * jc : (h + 1) * jc]))
-            a_ps = ps.tile([P, jh], F32, name="a_ps%d" % h)
             nc.tensor.matmul_mx(
-                a_ps[:],
+                a_ps[:, cols],
                 lhsT=w_codes[:].bitcast(FP8X4),
                 lhsT_scale=w_scales[:],
                 rhs=tab_gw[:, cols].bitcast(FP8X4),
@@ -117,11 +115,11 @@ def tile_attend_tcpickcentred_kernel(
                 start=True,
                 stop=True,
             )
-            nc.scalar.activation(h0[:, cols], a_ps[:], ACT.Tanh)
+            nc.scalar.activation(h0[:, cols], a_ps[:, cols], ACT.Tanh)
             nc.scalar.mul(h1[:, cols], h0[:, cols], gain_c[:])
 
         h0_sq = sb.tile([P, J], F32, name="h0_sq")
-        slope = sb.tile([P, J], F32, name="slope")
+        slope = sb.tile([P, J], F32, name="slope", tag="slope")
         nc.scalar.activation(h0_sq[:], h0[:], ACT.Square)
         nc.scalar.activation(slope[:], h0_sq[:], ACT.Identity, bias=gain_c[:], scale=neg_gain[:])
         centre = sb.tile([P, 1], F32, name="centre")
@@ -133,58 +131,52 @@ def tile_attend_tcpickcentred_kernel(
             return t.rearrange("p (g e) -> p g e", e=GROUP)
 
         nc.vector.tensor_copy(dtab_gs[:], dtab_s[:].indirect(slots[:]))
-        s = sb.tile([P, M], F32, name="s", tag="dtab_s", align_bytes=64)
-        nc.vector.tensor_tensor(s[:], h1[:].indirect(picks[:]), pb_t[:], ALU.add)
-        s_sum = sb.tile([P, G], F32, name="s_sum")
-        ta_ps = []
-        for h in range(HALVES):
-            slot_cols = slice(h * jh, (h + 1) * jh)
-            nc.vector.tensor_copy(dtab_gw[:, slot_cols], dtab_w[:].indirect(slots[:, h * jc : (h + 1) * jc]))
-            ta_ps.append(ps.tile([P, jh], F32, name="ta_ps%d" % h))
-            nc.tensor.matmul_mx(
-                ta_ps[h][:],
-                lhsT=w_codes[:].bitcast(FP8X4),
-                lhsT_scale=w_scales[:],
-                rhs=dtab_gw[:, slot_cols].bitcast(FP8X4),
-                rhs_scale=dtab_gs[DTAB_PLANE:P, slot_cols],
-                start=True,
-                stop=True,
-            )
-            if h == 0:
-                nc.vector.tensor_reduce(s_sum[:], grouped(s[:]), AXIS.X, ALU.add)
-
-        z = sb.tile([P, M], F32, name="z", tag="dtab_w")
-        nc.vector.scalar_tensor_tensor(
-            grouped(z[:]), s_sum[:].unsqueeze(2).to_broadcast([P, G, GROUP]), centre[:], grouped(s[:]), ALU.mult, ALU.add
+        dtab_gw = sb.tile([P, J], U32, name="dtab_gw", tag="dtab_s", align_bytes=64)
+        nc.vector.tensor_copy(dtab_gw[:], dtab_w[:].indirect(slots[:]))
+        ta_ps = ps.tile([P, J], F32, name="ta_ps")
+        nc.tensor.matmul_mx(
+            ta_ps[:],
+            lhsT=w_codes[:].bitcast(FP8X4),
+            lhsT_scale=w_scales[:],
+            rhs=dtab_gw[:].bitcast(FP8X4),
+            rhs_scale=dtab_gs[DTAB_PLANE:P, :],
+            start=True,
+            stop=True,
         )
-        th = sb.tile([P, M], F32, name="th")
-        nc.scalar.activation(th[:], z[:], ACT.Tanh, scale=0.5)
-
+        s = sb.tile([P, M], F32, name="s", tag="dtab_w")
+        nc.vector.tensor_tensor(s[:], h1[:].indirect(picks[:]), pb_t[:], ALU.add)
         xh1 = sb.tile([P, J], F32, name="xh1")
-        for h in range(HALVES):
-            slot_cols = slice(h * jh, (h + 1) * jh)
-            nc.vector.tensor_tensor(xh1[:, slot_cols], ta_ps[h][:], slope[:, slot_cols], ALU.mult)
+        nc.vector.tensor_tensor(xh1[:], ta_ps[:], slope[:], ALU.mult)
+        s_sum = sb.tile([P, G], F32, name="s_sum", tag="slope")
+        nc.vector.tensor_reduce(s_sum[:], grouped(s[:]), AXIS.X, ALU.add)
 
         mh = M // HALVES
         mc = mh // LIST_ROWS
         gh = G // HALVES
         cols = [slice(h * mh, (h + 1) * mh) for h in range(HALVES)]
         grps = [slice(h * gh, (h + 1) * gh) for h in range(HALVES)]
-        xs = sb.tile([P, M], F32, name="xs")
-        xs_sum = sb.tile([P, G], F32, name="xs_sum")
+        xs = [sb.tile([P, mh], F32, name="xs0")]
         xc = sb.tile([P, M], F32, name="xc")
         xg = sb.tile([P, M], F32, name="xg")
         res = sb.tile([P, M], F32, name="res")
+        nc.vector.tensor_copy(xs[0][:], xh1[:].indirect(picks[:, 0:mc]))
+        z = sb.tile([P, M], F32, name="z")
+        nc.vector.scalar_tensor_tensor(
+            grouped(z[:]), s_sum[:].unsqueeze(2).to_broadcast([P, G, GROUP]), centre[:], grouped(s[:]), ALU.mult, ALU.add
+        )
+        th = sb.tile([P, M], F32, name="th")
+        nc.scalar.activation(th[:], z[:], ACT.Tanh, scale=0.5)
+        xs.append(sb.tile([P, mh], F32, name="xs1", tag="slope"))
+        nc.vector.tensor_copy(xs[1][:], xh1[:].indirect(picks[:, mc : 2 * mc]))
+        xs_sum = sb.tile([P, G], F32, name="xs_sum")
         for h in range(HALVES):
-            nc.vector.tensor_copy(xs[:, cols[h]], xh1[:].indirect(picks[:, h * mc : (h + 1) * mc]))
-        for h in range(HALVES):
-            nc.vector.tensor_reduce(xs_sum[:, grps[h]], grouped(xs[:, cols[h]]), AXIS.X, ALU.add)
+            nc.vector.tensor_reduce(xs_sum[:, grps[h]], grouped(xs[h][:]), AXIS.X, ALU.add)
         for h in range(HALVES):
             nc.vector.scalar_tensor_tensor(
                 grouped(xc[:, cols[h]]),
                 xs_sum[:, grps[h]].unsqueeze(2).to_broadcast([P, gh, GROUP]),
                 centre[:],
-                grouped(xs[:, cols[h]]),
+                grouped(xs[h][:]),
                 ALU.mult,
                 ALU.add,
             )

@@ -92,7 +92,7 @@ def tile_attend_tcpickcentred_kernel(
 
         tab_gw = sb.tile([P, J], U32, name="tab_gw", align_bytes=64)
         tab_gs = sb.tile([P, J], U8, name="tab_gs", align_bytes=64)
-        dtab_gs = sb.tile([P, J], U8, name="dtab_gs", align_bytes=64)
+        dtab_gs = sb.tile([P, J], U8, name="dtab_gs", tag="dtab_gs", align_bytes=64)
 
         jh = J // HALVES
         jc = jh // LIST_ROWS
@@ -119,7 +119,7 @@ def tile_attend_tcpickcentred_kernel(
             nc.scalar.mul(h1[:, cols], h0[:, cols], gain_c[:])
 
         h0_sq = sb.tile([P, J], F32, name="h0_sq")
-        slope = sb.tile([P, J], F32, name="slope", tag="slope")
+        slope = sb.tile([P, J], F32, name="slope")
         nc.scalar.activation(h0_sq[:], h0[:], ACT.Square)
         nc.scalar.activation(slope[:], h0_sq[:], ACT.Identity, bias=gain_c[:], scale=neg_gain[:])
         centre = sb.tile([P, 1], F32, name="centre")
@@ -147,7 +147,7 @@ def tile_attend_tcpickcentred_kernel(
         nc.vector.tensor_tensor(s[:], h1[:].indirect(picks[:]), pb_t[:], ALU.add)
         xh1 = sb.tile([P, J], F32, name="xh1")
         nc.vector.tensor_tensor(xh1[:], ta_ps[:], slope[:], ALU.mult)
-        s_sum = sb.tile([P, G], F32, name="s_sum", tag="slope")
+        s_sum = sb.tile([P, G], F32, name="s_sum", tag="dtab_gs", align_bytes=64)
         nc.vector.tensor_reduce(s_sum[:], grouped(s[:]), AXIS.X, ALU.add)
 
         mh = M // HALVES
@@ -155,28 +155,27 @@ def tile_attend_tcpickcentred_kernel(
         gh = G // HALVES
         cols = [slice(h * mh, (h + 1) * mh) for h in range(HALVES)]
         grps = [slice(h * gh, (h + 1) * gh) for h in range(HALVES)]
-        xs = [sb.tile([P, mh], F32, name="xs0")]
+        xs = sb.tile([P, M], F32, name="xs")
         xc = sb.tile([P, M], F32, name="xc")
         xg = sb.tile([P, M], F32, name="xg")
         res = sb.tile([P, M], F32, name="res")
-        nc.vector.tensor_copy(xs[0][:], xh1[:].indirect(picks[:, 0:mc]))
+        nc.vector.tensor_copy(xs[:, cols[0]], xh1[:].indirect(picks[:, 0:mc]))
         z = sb.tile([P, M], F32, name="z")
         nc.vector.scalar_tensor_tensor(
             grouped(z[:]), s_sum[:].unsqueeze(2).to_broadcast([P, G, GROUP]), centre[:], grouped(s[:]), ALU.mult, ALU.add
         )
         th = sb.tile([P, M], F32, name="th")
         nc.scalar.activation(th[:], z[:], ACT.Tanh, scale=0.5)
-        xs.append(sb.tile([P, mh], F32, name="xs1", tag="slope"))
-        nc.vector.tensor_copy(xs[1][:], xh1[:].indirect(picks[:, mc : 2 * mc]))
+        nc.vector.tensor_copy(xs[:, cols[1]], xh1[:].indirect(picks[:, mc : 2 * mc]))
         xs_sum = sb.tile([P, G], F32, name="xs_sum")
         for h in range(HALVES):
-            nc.vector.tensor_reduce(xs_sum[:, grps[h]], grouped(xs[h][:]), AXIS.X, ALU.add)
+            nc.vector.tensor_reduce(xs_sum[:, grps[h]], grouped(xs[:, cols[h]]), AXIS.X, ALU.add)
         for h in range(HALVES):
             nc.vector.scalar_tensor_tensor(
                 grouped(xc[:, cols[h]]),
                 xs_sum[:, grps[h]].unsqueeze(2).to_broadcast([P, gh, GROUP]),
                 centre[:],
-                grouped(xs[h][:]),
+                grouped(xs[:, cols[h]]),
                 ALU.mult,
                 ALU.add,
             )

@@ -58,7 +58,7 @@ def tile_attend_tcpickcentred_kernel(
         base_t = sb.tile([P, M], F32, name="base_t")
         ident = sb.tile([P, P], F32, name="ident")
 
-        nc.gpsimd.memset(tab_s[:].bitcast(I32), 0)
+        nc.vector.memset(tab_s[:].bitcast(I32), 0)
         nc.vector.memset(dtab_s[:].bitcast(I32), 0)
 
         make_identity(nc, ident[:])

from contextlib import ExitStack

import concourse.mybir as mybir
from concourse.masks import make_identity

K, R, T, J, M, G = 512, 128, 2048, 512, 256, 32
FLOPS = 2 * 2 * K * R * J

F32 = mybir.dt.float32
BF16 = mybir.dt.bfloat16
I32 = mybir.dt.int32
U32 = mybir.dt.uint32
U16 = mybir.dt.uint16
U8 = mybir.dt.uint8
FP8X4 = mybir.dt.float8_e4m3fn_x4
ALU = mybir.AluOpType
ACT = mybir.ActivationFunctionType
AXIS = mybir.AxisListType

P = 128
PACK = 4
GROUP = M // G
LIST_ROWS = 16
TAB_PLANE = 0
DTAB_PLANE = 4
HALVES = 2


def load_words(nc, tile, words):
    nc.sync.dma_start(tile[:].bitcast(I32), words[0].rearrange("p n t -> p (n t)").bitcast(I32))


def load_scales(queues, tile, scales, plane):
    for q, queue in enumerate(queues):
        first = 32 * q + plane
        queue.dma_start(tile[first : first + 4, :].bitcast(I32), scales[0, 4 * q : 4 * q + 4, :].bitcast(I32))


def tile_attend_tcpickcentred_kernel(
    tc, dtab_words, dtab_scales, tab_words, tab_scales, w1, gain, share, pb, og, base, offs, offs2, out
):
    nc = tc.nc
    with ExitStack() as ctx:
        sb = ctx.enter_context(tc.tile_pool(name="sb", bufs=1))
        ps = ctx.enter_context(tc.psum_pool(name="ps", bufs=1))

        slots = sb.tile([P, J // LIST_ROWS], U16, name="slots")
        picks = sb.tile([P, M // LIST_ROWS], U16, name="picks")
        tab_w = sb.tile([P, T], U32, name="tab_w")
        tab_s = sb.tile([P, T], U8, name="tab_s")
        dtab_w = sb.tile([P, T], U32, name="dtab_w", tag="dtab_w")
        dtab_s = sb.tile([P, T], U8, name="dtab_s", tag="dtab_s", align_bytes=64)
        w_raw = sb.tile([P, PACK, R], F32, name="w_raw")
        gain_c = sb.tile([P, 1], F32, name="gain_c")
        share_c = sb.tile([P, 1], F32, name="share_c")
        og_c = sb.tile([P, 1], F32, name="og_c")
        pb_c = sb.tile([P, 2], F32, name="pb_c")
        base_t = sb.tile([P, M], F32, name="base_t")
        ident = sb.tile([P, P], F32, name="ident")

        nc.vector.memset(tab_s[:].bitcast(I32), 0)
        nc.vector.memset(dtab_s[:].bitcast(I32), 0)

        make_identity(nc, ident[:])
        nc.sync.dma_start(slots[:], offs)
        nc.sync.dma_start(w_raw[:], w1.rearrange("(p j) r -> p j r", j=PACK))
        nc.scalar.dma_start(pb_c[:], pb.rearrange("o (p c) -> p (o c)", c=2))
        load_scales([nc.sync, nc.sync, nc.scalar, nc.scalar], tab_s, tab_scales, TAB_PLANE)
        load_words(nc, tab_w, tab_words)
        nc.sync.dma_start(gain_c[:], gain)
        load_scales([nc.sync] * 4, dtab_s, dtab_scales, DTAB_PLANE)
        load_words(nc, dtab_w, dtab_words)
        nc.sync.dma_start(picks[:], offs2)
        nc.sync.dma_start(share_c[:], share)
        nc.sync.dma_start(og_c[:], og)
        nc.sync.dma_start(base_t[:], base)

        w_bf = sb.tile([P, R, PACK], BF16, name="w_bf", align_bytes=64)
        nc.vector.tensor_copy(w_bf[:], w_raw[:].rearrange("p j r -> p r j"))

        pb_ps = ps.tile([P, 2, P], F32, name="pb_ps", tag="bank0")
        for c in range(2):
            nc.tensor.transpose(pb_ps[:, c, :], pb_c[:, c : c + 1].to_broadcast([P, P]), ident[:])
        pb_t = sb.tile([P, M], F32, name="pb_t")
        nc.scalar.copy(pb_t[:].rearrange("p (n c) -> p n c", c=2), pb_ps[:].rearrange("p c n -> p n c"))

        neg_gain = sb.tile([P, 1], F32, name="neg_gain")
        nc.scalar.mul(neg_gain[:], gain_c[:], -1.0)

        w_codes = sb.tile([P, R], U32, name="w_codes", align_bytes=64)
        w_scales = sb.tile([P, R], U8, name="w_scales", align_bytes=64)

        tab_gw = sb.tile([P, J], U32, name="tab_gw", align_bytes=64)
        tab_gs = sb.tile([P, J], U8, name="tab_gs", align_bytes=64)
        dtab_gs = sb.tile([P, J], U8, name="dtab_gs", tag="dtab_gs", align_bytes=64)

        jh = J // HALVES
        jc = jh // LIST_ROWS
        nc.vector.quantize_mx(
            out=w_codes[:].bitcast(FP8X4), scales=w_scales[:], in_=w_bf[:].rearrange("p r j -> p (r j)")
        )
        nc.vector.tensor_copy(tab_gs[:], tab_s[:].indirect(slots[:]))
        a_ps = ps.tile([P, J], F32, name="a_ps", tag="bank0")
        h0 = sb.tile([P, J], F32, name="h0")
        h1 = sb.tile([P, J], F32, name="h1")
        for h in range(HALVES):
            cols = slice(h * jh, (h + 1) * jh)
            nc.vector.tensor_copy(tab_gw[:, cols], tab_w[:].indirect(slots[:, h * jc : (h + 1) * jc]))
            nc.tensor.matmul_mx(
                a_ps[:, cols],
                lhsT=w_codes[:].bitcast(FP8X4),
                lhsT_scale=w_scales[:],
                rhs=tab_gw[:, cols].bitcast(FP8X4),
                rhs_scale=tab_gs[TAB_PLANE:P, cols],
                start=True,
                stop=True,
            )
            nc.scalar.activation(h0[:, cols], a_ps[:, cols], ACT.Tanh)
            nc.scalar.mul(h1[:, cols], h0[:, cols], gain_c[:])

        h0_sq = sb.tile([P, J], F32, name="h0_sq")
        slope = sb.tile([P, J], F32, name="slope")
        nc.scalar.activation(h0_sq[:], h0[:], ACT.Square)
        nc.scalar.activation(slope[:], h0_sq[:], ACT.Identity, bias=gain_c[:], scale=neg_gain[:])
        centre = sb.tile([P, 1], F32, name="centre")
        nc.scalar.mul(centre[:], share_c[:], -1.0 / GROUP)
        half_og = sb.tile([P, 1], F32, name="half_og")
        nc.scalar.mul(half_og[:], og_c[:], 0.5)

        def grouped(t):
            return t.rearrange("p (g e) -> p g e", e=GROUP)

        nc.vector.tensor_copy(dtab_gs[:], dtab_s[:].indirect(slots[:]))
        dtab_gw = sb.tile([P, J], U32, name="dtab_gw", tag="dtab_s", align_bytes=64)
        nc.vector.tensor_copy(dtab_gw[:], dtab_w[:].indirect(slots[:]))
        ta_ps = ps.tile([P, J], F32, name="ta_ps")
        nc.tensor.matmul_mx(
            ta_ps[:],
            lhsT=w_codes[:].bitcast(FP8X4),
            lhsT_scale=w_scales[:],
            rhs=dtab_gw[:].bitcast(FP8X4),
            rhs_scale=dtab_gs[DTAB_PLANE:P, :],
            start=True,
            stop=True,
        )
        s = sb.tile([P, M], F32, name="s", tag="dtab_w")
        nc.vector.tensor_tensor(s[:], h1[:].indirect(picks[:]), pb_t[:], ALU.add)
        xh1 = sb.tile([P, J], F32, name="xh1")
        nc.vector.tensor_tensor(xh1[:], ta_ps[:], slope[:], ALU.mult)
        s_sum = sb.tile([P, G], F32, name="s_sum", tag="dtab_gs", align_bytes=64)
        nc.vector.tensor_reduce(s_sum[:], grouped(s[:]), AXIS.X, ALU.add)

        mh = M // HALVES
        mc = mh // LIST_ROWS
        gh = G // HALVES
        cols = [slice(h * mh, (h + 1) * mh) for h in range(HALVES)]
        grps = [slice(h * gh, (h + 1) * gh) for h in range(HALVES)]
        xs = sb.tile([P, M], F32, name="xs")
        xc = sb.tile([P, M], F32, name="xc")
        xg = sb.tile([P, M], F32, name="xg")
        res = sb.tile([P, M], F32, name="res")
        nc.vector.tensor_copy(xs[:, cols[0]], xh1[:].indirect(picks[:, 0:mc]))
        z = sb.tile([P, M], F32, name="z")
        nc.vector.scalar_tensor_tensor(
            grouped(z[:]), s_sum[:].unsqueeze(2).to_broadcast([P, G, GROUP]), centre[:], grouped(s[:]), ALU.mult, ALU.add
        )
        th = sb.tile([P, M], F32, name="th")
        nc.scalar.activation(th[:], z[:], ACT.Tanh, scale=0.5)
        nc.vector.tensor_copy(xs[:, cols[1]], xh1[:].indirect(picks[:, mc : 2 * mc]))
        xs_sum = sb.tile([P, G], F32, name="xs_sum")
        for h in range(HALVES):
            nc.vector.tensor_reduce(xs_sum[:, grps[h]], grouped(xs[:, cols[h]]), AXIS.X, ALU.add)
        for h in range(HALVES):
            nc.vector.scalar_tensor_tensor(
                grouped(xc[:, cols[h]]),
                xs_sum[:, grps[h]].unsqueeze(2).to_broadcast([P, gh, GROUP]),
                centre[:],
                grouped(xs[:, cols[h]]),
                ALU.mult,
                ALU.add,
            )
        for h in range(HALVES):
            nc.vector.scalar_tensor_tensor(xg[:, cols[h]], th[:, cols[h]], 1.0, xc[:, cols[h]], ALU.add, ALU.mult)
        for h in range(HALVES):
            nc.vector.scalar_tensor_tensor(
                res[:, cols[h]], xg[:, cols[h]], half_og[:], base_t[:, cols[h]], ALU.mult, ALU.add
            )
            queue = nc.sync if h == 0 else nc.scalar
            queue.dma_start(out[:, cols[h]], res[:, cols[h]])
